import numpy as np
import ml_dtypes


def mxq(x, axis, fmt="e4m3"):
    dtype, down = {"e4m3": (ml_dtypes.float8_e4m3fn, 7), "e5m2": (ml_dtypes.float8_e5m2, 14)}[fmt]
    v = np.moveaxis(np.asarray(x, np.float32).astype(ml_dtypes.bfloat16).astype(np.float64), axis, -1)
    blocks = v.reshape(v.shape[:-1] + (-1, 32))
    amax = np.abs(blocks).max(-1, keepdims=True)
    byte = np.maximum(np.where(amax > 0, np.frexp(amax)[1] - 1 + 127, 0) - down, 1)
    scale = np.exp2(byte - 127.0)
    codes = (blocks / scale).astype(np.float32).astype(dtype).astype(np.float64)
    return np.moveaxis((codes * scale).reshape(v.shape), -1, axis)


WIDE = False


def mx_kscale(k):
    if not WIDE:
        return np.ones(k)
    levels = np.array([10, -10, 5, -5, 0])
    if k % 512:
        return np.exp2(np.random.permutation(np.resize(levels, k // 32))).repeat(32)
    a = np.empty((k // 512, 16))
    for p in range(k // 512):
        a[p, :8] = np.random.permutation(np.resize(levels, 8))
        for g in range(8):
            far = levels[np.abs(levels - a[p, g]) >= 10]
            a[p, g + 8] = far[np.random.randint(len(far))]
    return np.exp2(a.ravel()).repeat(32)


BF16 = ml_dtypes.bfloat16


def bf(x):
    return np.asarray(x, np.float32).astype(BF16)


def f64(x):
    return np.asarray(x).astype(np.float64)


E2M1 = np.array([0.0, 0.5, 1.0, 1.5, 2.0, 3.0, 4.0, 6.0, -0.0, -0.5, -1.0, -1.5, -2.0, -3.0, -4.0, -6.0])


def pack_weight(w, fmt):
    k, n = w.shape
    w = f64(bf(w)).reshape(k // 32, 32, n)
    amax = np.abs(w).max(1)
    if fmt == "e4m3":
        byte = np.frexp(amax)[1] - 1 + 127 - 7
    else:
        mant, ex = np.frexp(amax / 6.0)
        byte = np.where(mant > 0.5, ex, ex - 1) + 127
    byte = np.clip(np.where(amax > 0, byte, 1), 1, 254)
    scaled = (w * np.exp2(127.0 - byte)[:, None, :]).reshape(k, n).astype(np.float32)
    by_word = np.ascontiguousarray(scaled.reshape(k // 512, 128, 4, n).transpose(0, 1, 3, 2))
    if fmt == "e4m3":
        words = by_word.astype(ml_dtypes.float8_e4m3fn).view(np.uint8)
    else:
        c = by_word.astype(ml_dtypes.float4_e2m1fn).view(np.uint8) & 0xF
        words = c[..., 0::2] | (c[..., 1::2] << 4)
    return np.ascontiguousarray(words), np.ascontiguousarray(byte.astype(np.uint8).reshape(k // 512, 16, n))


def unpack_weight(words, scales, fmt):
    g, p, n, _ = words.shape
    if fmt == "e4m3":
        vals = np.ascontiguousarray(words).view(ml_dtypes.float8_e4m3fn).astype(np.float64)
    else:
        nib = np.empty((g, p, n, 4), np.uint8)
        nib[..., 0::2] = words & 0xF
        nib[..., 1::2] = words >> 4
        vals = E2M1[nib]
    vals = vals * np.repeat(np.exp2(scales.astype(np.float64) - 127.0), 8, axis=1)[..., None]
    return vals.transpose(0, 1, 3, 2).reshape(g * 512, n)
def pack4(w):
    words, scales = pack_weight(w, "e2m1")
    return words.reshape(words.shape[0], 128, -1), scales


def unpack4(words, scales):
    return unpack_weight(words.reshape(words.shape[0], 128, -1, 2), scales, "e2m1")


M, K, N = 2048, 1024, 1024


def setup_inputs():
    s = mx_kscale(K)
    x = np.random.standard_normal((M, K)) * s
    style_root = np.random.standard_normal((K, N)) / np.sqrt(K) / s[:, None]
    content_root = np.random.standard_normal((K, N)) / np.sqrt(K) / s[:, None]
    style_words, style_scales = pack4(style_root)
    return {"x": bf(x),
            "strength": bf(np.random.uniform(0.2, 0.8, M)),
            "style_words": style_words,
            "style_scales": style_scales,
            "content_root": bf(content_root),
            "style_mean": bf(0.5 * np.random.standard_normal(N))}


def reference(x, strength, style_words, style_scales, content_root, style_mean):
    z = f64(x)
    a = f64(strength)[:, None]
    b = 1.0 - a
    styled = mxq(z * a, 1, "e4m3")
    kept = mxq(z * b, 1, "e4m3")
    v = unpack4(style_words, style_scales)
    c = mxq(f64(content_root), 0, "e4m3")
    y = (styled @ v) + (kept @ c)
    return y + a * f64(style_mean)

@@ -1,0 +1,276 @@
+from contextlib import ExitStack
+
+import concourse.mybir as mybir
+from concourse.masks import make_identity
+
+M, K, N = 2048, 1024, 1024
+FLOPS = 2 * 2 * M * K * N
+
+F32 = mybir.dt.float32
+BF16 = mybir.dt.bfloat16
+I32 = mybir.dt.int32
+U32 = mybir.dt.uint32
+U8 = mybir.dt.uint8
+FP8X4 = mybir.dt.float8_e4m3fn_x4
+FP4X4 = mybir.dt.float4_e2m1fn_x4
+ALU = mybir.AluOpType
+
+P = 128
+PACK = 4
+K_PASS = P * PACK
+PASSES = K // K_PASS
+TILES = M // P
+N_HALF = 512
+HALVES = N // N_HALF
+STYLED, KEPT = 0, 1
+LEAD = 8
+HEAD_VECTOR_COLS = 336
+LATE_PIECE_COLS = 128
+
+
+def tile_whitening_colouring_blend_s1_kernel(
+    tc, x, strength, style_words, style_scales, content_root, style_mean, out
+):
+    nc = tc.nc
+    x_rows = x.rearrange("(p i) k -> p i k", i=TILES)
+    out_rows = out.rearrange("(p i) n -> p i n", i=TILES)
+
+    with ExitStack() as ctx:
+        keep = ctx.enter_context(tc.tile_pool(name="keep", bufs=1))
+        stage = ctx.enter_context(tc.tile_pool(name="stage", bufs=4))
+        psum = ctx.enter_context(tc.psum_pool(name="psum", bufs=1))
+        ctx.enter_context(tc.manual_schedule())
+
+        ident = keep.tile([P, P], F32, name="ident")
+        make_identity(nc, ident[:])
+
+        v_scales = keep.tile([P, PASSES, N], U8, name="v_scales", align_bytes=64)
+        nc.vector.memset(v_scales[:].rearrange("p g n -> p (g n)").bitcast(I32), 0)
+
+        a_bf = keep.tile([P, TILES], BF16, name="a_bf")
+        mean_part = keep.tile([P, N // P], BF16, name="mean_part")
+        x_sb = {}
+        c_raw = {}
+        v_words = {}
+
+        def load_x(first, count):
+            t = keep.tile([P, count * K], BF16, name="x_%d" % first)
+            nc.sync.dma_start(out=t[:], in_=x_rows[:, first : first + count, :].rearrange("p i k -> p (i k)"))
+            for i in range(count):
+                x_sb[first + i] = t[:, i * K : (i + 1) * K]
+
+        def load_c(g, h):
+            t = keep.tile([P, PACK, N_HALF], BF16, name="c_raw_%d_%d" % (g, h))
+            rows = content_root[g * K_PASS : (g + 1) * K_PASS, h * N_HALF : (h + 1) * N_HALF]
+            nc.sync.dma_start(out=t[:], in_=rows.rearrange("(p t) n -> p t n", t=PACK))
+            c_raw[g, h] = t
+
+        def load_v(h):
+            t = keep.tile([P, PASSES, 2 * N_HALF], U8, name="v_words_%d" % h, align_bytes=64)
+            width = N_HALF // 2
+            src = style_words.bitcast(I32)[:, :, h * width : (h + 1) * width]
+            nc.sync.dma_start(out=t[:].bitcast(I32), in_=src.rearrange("g p w -> p g w"))
+            v_words[h] = t
+
+        nc.sync.dma_start(out=a_bf[:], in_=strength.rearrange("(p i) -> p i", i=TILES))
+        load_x(0, 1)
+        load_c(0, 0)
+        for q in range(4):
+            src = style_scales.bitcast(I32)[:, 4 * q : 4 * q + 4, :]
+            nc.sync.dma_start(out=v_scales[32 * q : 32 * q + 4, :, :].bitcast(I32), in_=src.rearrange("g r w -> r g w"))
+        nc.sync.dma_start(out=mean_part[:], in_=style_mean.rearrange("(p c) -> p c", p=P))
+        load_x(1, 1)
+        load_v(0)
+        load_c(1, 0)
+        load_x(2, 1)
+        load_x(3, 1)
+        load_c(0, 1)
+        load_x(4, 2)
+        load_c(1, 1)
+        load_x(6, 2)
+        load_v(1)
+        for first in range(8, TILES, 4):
+            load_x(first, 4)
+
+        share = keep.tile([P, 2, TILES], F32, name="share")
+        nc.vector.tensor_copy(out=share[:, STYLED, :], in_=a_bf[:])
+        nc.vector.tensor_scalar(
+            out=share[:, KEPT, :], in0=a_bf[:], scalar1=-1.0, scalar2=1.0, op0=ALU.mult, op1=ALU.add
+        )
+
+        mean_all = keep.tile([P, N], BF16, name="mean_all")
+        c_grouped = {}
+        c_codes = {}
+        c_scales = {}
+        for g in range(PASSES):
+            for h in range(HALVES):
+                c_grouped[g, h] = keep.tile([P, N_HALF * PACK], BF16, name="c_grouped_%d_%d" % (g, h), align_bytes=64)
+                c_codes[g, h] = keep.tile([P, N_HALF], U32, name="c_codes_%d_%d" % (g, h), align_bytes=64)
+                c_scales[g, h] = keep.tile([P, N_HALF], U8, name="c_scales_%d_%d" % (g, h), align_bytes=64)
+        x_codes = {}
+        x_scales = {}
+        for i in range(TILES):
+            x_codes[i] = keep.tile([P, 2 * PASSES * P], U32, name="x_codes_%d" % i, align_bytes=64)
+            x_scales[i] = keep.tile([P, 2 * PASSES * P], U8, name="x_scales_%d" % i, align_bytes=64)
+
+        scaled = {}
+        turned = {}
+        acc = {}
+        opened = []
+
+        def spread_mean():
+            bank = psum.tile([P, N_HALF], F32, name="mean_bank", tag="acc3")
+            words = mean_part[:].bitcast(F32)
+            for c in range(4):
+                nc.tensor.transpose(bank[:, c * P : (c + 1) * P], words[:, c : c + 1].to_broadcast([P, P]), ident[:])
+            nc.scalar.copy(
+                out=mean_all[:].bitcast(F32).rearrange("p (j c) -> p j c", c=4),
+                in_=bank[:].rearrange("p (c j) -> p j c", c=4),
+            )
+
+        def interleave_c(engine_copy, g, h, col0, col1):
+            dst = c_grouped[g, h][:, col0 * PACK : col1 * PACK].rearrange("p (c i t) -> p c t i", i=4, t=PACK)
+            src = c_raw[g, h][:, :, col0:col1].rearrange("p t (c i) -> p c t i", i=4)
+            engine_copy(out=dst, in_=src)
+
+        def quantise_c(g, h):
+            nc.vector.quantize_mx(out=c_codes[g, h][:].bitcast(FP8X4), scales=c_scales[g, h][:], in_=c_grouped[g, h][:])
+
+        def scale(i):
+            for o in (STYLED, KEPT):
+                t = stage.tile([P, K], BF16, name="scaled", tag="scaled%d" % o)
+                nc.vector.tensor_scalar(
+                    out=t[:].rearrange("p (u w e) -> p u w e", u=2, e=2),
+                    in0=x_sb[i].rearrange("p (w u e) -> p u w e", u=2, e=2),
+                    scalar1=share[:, o, i : i + 1],
+                    scalar2=None,
+                    op0=ALU.mult,
+                )
+                scaled[i, o] = t
+
+        def turn(tiles):
+            banks = {}
+            for i in tiles:
+                for o in (STYLED, KEPT):
+                    bank = psum.tile([P, N_HALF], F32, name="turn_bank", tag="turn%d" % (2 * (i % 2) + o))
+                    words = scaled[i, o][:].bitcast(F32)
+                    for s in range(4):
+                        nc.tensor.transpose(bank[:, s * P : (s + 1) * P], words[:, s * P : (s + 1) * P], ident[:])
+                    banks[i, o] = bank
+            for i in tiles:
+                t = stage.tile([P, 2 * K], BF16, name="turned", tag="turned", align_bytes=64)
+                for o in (STYLED, KEPT):
+                    nc.scalar.copy(
+                        out=t[:, o * K : (o + 1) * K].bitcast(F32).rearrange("p (g r u) -> p g r u", g=PASSES, u=2),
+                        in_=banks[i, o][:].rearrange("p (u g r) -> p g r u", u=2, g=PASSES),
+                    )
+                turned[i] = t
+
+        def quantise_x(i):
+            nc.vector.quantize_mx(out=x_codes[i][:].bitcast(FP8X4), scales=x_scales[i][:], in_=turned[i][:])
+
+        def multiply(i, h, o):
+            if o == STYLED:
+                acc[i, h] = psum.tile([P, N_HALF], F32, name="acc", tag="acc%d" % (len(opened) % 4))
+                opened.append((i, h))
+            for g in range(PASSES):
+                cols = slice((o * PASSES + g) * P, (o * PASSES + g + 1) * P)
+                if o == STYLED:
+                    rhs = v_words[h][:, g, :].bitcast(FP4X4)
+                    rhs_scale = v_scales[:, g, h * N_HALF : (h + 1) * N_HALF]
+                else:
+                    rhs = c_codes[g, h][:].bitcast(FP8X4)
+                    rhs_scale = c_scales[g, h][:]
+                nc.tensor.matmul_mx(
+                    out=acc[i, h][:],
+                    lhsT=x_codes[i][:, cols].bitcast(FP8X4),
+                    lhsT_scale=x_scales[i][:, cols],
+                    rhs=rhs,
+                    rhs_scale=rhs_scale,
+                    start=(o == STYLED and g == 0),
+                    stop=(o == KEPT and g == PASSES - 1),
+                )
+
+        def unit(i, h):
+            multiply(i, h, STYLED)
+            multiply(i, h, KEPT)
+
+        def finish(i, h):
+            cols = slice(h * N_HALF, (h + 1) * N_HALF)
+            t = stage.tile([P, N_HALF], F32, name="result", tag="result", bufs=8)
+            nc.vector.scalar_tensor_tensor(
+                out=t[:],
+                in0=mean_all[:, cols],
+                scalar=share[:, STYLED, i : i + 1],
+                in1=acc[i, h][:],
+                op0=ALU.mult,
+                op1=ALU.add,
+            )
+            nc.sync.dma_start(out=out_rows[:, i, cols], in_=t[:])
+
+        scale(0)
+        turn([0])
+        interleave_c(nc.vector.tensor_copy, 0, 0, 0, HEAD_VECTOR_COLS)
+        interleave_c(nc.scalar.copy, 0, 0, HEAD_VECTOR_COLS, N_HALF)
+        scale(1)
+        turn([1])
+        quantise_x(0)
+        quantise_c(0, 0)
+        quantise_x(1)
+        interleave_c(nc.vector.tensor_copy, 1, 0, 0, HEAD_VECTOR_COLS)
+        interleave_c(nc.scalar.copy, 1, 0, HEAD_VECTOR_COLS, N_HALF)
+        multiply(0, 0, STYLED)
+        multiply(1, 0, STYLED)
+        scale(2)
+        spread_mean()
+        turn([2])
+        quantise_c(1, 0)
+        multiply(0, 0, KEPT)
+        multiply(1, 0, KEPT)
+        scale(3)
+        quantise_x(2)
+        finish(0, 0)
+
+        pieces = [(g, c) for g in range(PASSES) for c in range(0, N_HALF, LATE_PIECE_COLS)]
+        steps = LEAD - 2
+        for j in range(2, LEAD):
+            turn([j + 1])
+            s = j - 2
+            mine = pieces[s * len(pieces) // steps : (s + 1) * len(pieces) // steps]
+            for g, c in mine:
+                interleave_c(nc.scalar.copy, g, 1, c, c + LATE_PIECE_COLS)
+            finish(j - 1, 0)
+            unit(j, 0)
+            scale(j + 2)
+            quantise_x(j + 1)
+            for g, c in mine:
+                if c + LATE_PIECE_COLS == N_HALF:
+                    quantise_c(g, 1)
+        scale(LEAD + 2)
+
+        last = (LEAD - 1, 0)
+        for j in range(LEAD, TILES, 2):
+            ahead = [i for i in (j + 1, j + 2) if i < TILES]
+            turn(ahead)
+            finish(*last)
+            unit(j, 0)
+            if j + 3 < TILES:
+                scale(j + 3)
+            quantise_x(j + 1)
+            finish(j, 0)
+            unit(j - LEAD, 1)
+            if j + 4 < TILES:
+                scale(j + 4)
+            if j + 2 < TILES:
+                quantise_x(j + 2)
+            unit(j + 1, 0)
+            finish(j - LEAD, 1)
+            unit(j + 1 - LEAD, 1)
+            finish(j + 1, 0)
+            last = (j + 1 - LEAD, 1)
+
+        for i in range(TILES - LEAD, TILES):
+            unit(i, 1)
+            finish(*last)
+            last = (i, 1)
+        finish(*last)

@@ -23,8 +23,9 @@ TILES = M // P
 N_HALF = 512
 HALVES = N // N_HALF
 STYLED, KEPT = 0, 1
-LEAD = 8
-HEAD_VECTOR_COLS = 336
+EARLY = 3
+LEAD = 6
+HEAD_VECTOR_COLS = 320
 LATE_PIECE_COLS = 128
 
 
@@ -74,21 +75,22 @@ def tile_whitening_colouring_blend_s1_kernel(
 
         nc.sync.dma_start(out=a_bf[:], in_=strength.rearrange("(p i) -> p i", i=TILES))
         load_x(0, 1)
-        load_c(0, 0)
+        load_x(1, 1)
+        load_v(0)
         for q in range(4):
             src = style_scales.bitcast(I32)[:, 4 * q : 4 * q + 4, :]
             nc.sync.dma_start(out=v_scales[32 * q : 32 * q + 4, :, :].bitcast(I32), in_=src.rearrange("g r w -> r g w"))
         nc.sync.dma_start(out=mean_part[:], in_=style_mean.rearrange("(p c) -> p c", p=P))
-        load_x(1, 1)
-        load_v(0)
-        load_c(1, 0)
+        load_c(0, 0)
+        load_v(1)
         load_x(2, 1)
+        load_c(1, 0)
         load_x(3, 1)
+        load_x(4, 1)
         load_c(0, 1)
-        load_x(4, 2)
+        load_x(5, 1)
         load_c(1, 1)
         load_x(6, 2)
-        load_v(1)
         for first in range(8, TILES, 4):
             load_x(first, 4)
 
@@ -116,10 +118,15 @@ def tile_whitening_colouring_blend_s1_kernel(
         scaled = {}
         turned = {}
         acc = {}
-        opened = []
+        acc_bank = {}
+        free_banks = list(range(8))
+
+        def take_bank():
+            b = free_banks.pop(0)
+            return b, psum.tile([P, N_HALF], F32, name="bank", tag="bank%d" % b)
 
         def spread_mean():
-            bank = psum.tile([P, N_HALF], F32, name="mean_bank", tag="acc3")
+            b, bank = take_bank()
             words = mean_part[:].bitcast(F32)
             for c in range(4):
                 nc.tensor.transpose(bank[:, c * P : (c + 1) * P], words[:, c : c + 1].to_broadcast([P, P]), ident[:])
@@ -127,6 +134,7 @@ def tile_whitening_colouring_blend_s1_kernel(
                 out=mean_all[:].bitcast(F32).rearrange("p (j c) -> p j c", c=4),
                 in_=bank[:].rearrange("p (c j) -> p j c", c=4),
             )
+            free_banks.append(b)
 
         def interleave_c(engine_copy, g, h, col0, col1):
             dst = c_grouped[g, h][:, col0 * PACK : col1 * PACK].rearrange("p (c i t) -> p c t i", i=4, t=PACK)
@@ -152,37 +160,37 @@ def tile_whitening_colouring_blend_s1_kernel(
             banks = {}
             for i in tiles:
                 for o in (STYLED, KEPT):
-                    bank = psum.tile([P, N_HALF], F32, name="turn_bank", tag="turn%d" % (2 * (i % 2) + o))
+                    b, bank = take_bank()
                     words = scaled[i, o][:].bitcast(F32)
                     for s in range(4):
                         nc.tensor.transpose(bank[:, s * P : (s + 1) * P], words[:, s * P : (s + 1) * P], ident[:])
-                    banks[i, o] = bank
+                    banks[i, o] = (b, bank)
             for i in tiles:
                 t = stage.tile([P, 2 * K], BF16, name="turned", tag="turned", align_bytes=64)
                 for o in (STYLED, KEPT):
                     nc.scalar.copy(
                         out=t[:, o * K : (o + 1) * K].bitcast(F32).rearrange("p (g r u) -> p g r u", g=PASSES, u=2),
-                        in_=banks[i, o][:].rearrange("p (u g r) -> p g r u", u=2, g=PASSES),
+                        in_=banks[i, o][1][:].rearrange("p (u g r) -> p g r u", u=2, g=PASSES),
                     )
+                    free_banks.append(banks[i, o][0])
                 turned[i] = t
 
         def quantise_x(i):
             nc.vector.quantize_mx(out=x_codes[i][:].bitcast(FP8X4), scales=x_scales[i][:], in_=turned[i][:])
 
-        def multiply(i, h, o):
+        def multiply(i, h, o, n0=0, n1=N_HALF):
             if o == STYLED:
-                acc[i, h] = psum.tile([P, N_HALF], F32, name="acc", tag="acc%d" % (len(opened) % 4))
-                opened.append((i, h))
+                acc_bank[i, h, n0], acc[i, h, n0] = take_bank()
             for g in range(PASSES):
                 cols = slice((o * PASSES + g) * P, (o * PASSES + g + 1) * P)
                 if o == STYLED:
-                    rhs = v_words[h][:, g, :].bitcast(FP4X4)
-                    rhs_scale = v_scales[:, g, h * N_HALF : (h + 1) * N_HALF]
+                    rhs = v_words[h][:, g, 2 * n0 : 2 * n1].bitcast(FP4X4)
+                    rhs_scale = v_scales[:, g, h * N_HALF + n0 : h * N_HALF + n1]
                 else:
-                    rhs = c_codes[g, h][:].bitcast(FP8X4)
-                    rhs_scale = c_scales[g, h][:]
+                    rhs = c_codes[g, h][:, n0:n1].bitcast(FP8X4)
+                    rhs_scale = c_scales[g, h][:, n0:n1]
                 nc.tensor.matmul_mx(
-                    out=acc[i, h][:],
+                    out=acc[i, h, n0][:, 0 : n1 - n0],
                     lhsT=x_codes[i][:, cols].bitcast(FP8X4),
                     lhsT_scale=x_scales[i][:, cols],
                     rhs=rhs,
@@ -191,51 +199,62 @@ def tile_whitening_colouring_blend_s1_kernel(
                     stop=(o == KEPT and g == PASSES - 1),
                 )
 
-        def unit(i, h):
-            multiply(i, h, STYLED)
-            multiply(i, h, KEPT)
+        def unit(i, h, n0=0, n1=N_HALF):
+            multiply(i, h, STYLED, n0, n1)
+            multiply(i, h, KEPT, n0, n1)
 
-        def finish(i, h):
-            cols = slice(h * N_HALF, (h + 1) * N_HALF)
+        def finish(i, h, n0=0, n1=N_HALF):
+            cols = slice(h * N_HALF + n0, h * N_HALF + n1)
             t = stage.tile([P, N_HALF], F32, name="result", tag="result", bufs=8)
             nc.vector.scalar_tensor_tensor(
-                out=t[:],
+                out=t[:, 0 : n1 - n0],
                 in0=mean_all[:, cols],
                 scalar=share[:, STYLED, i : i + 1],
-                in1=acc[i, h][:],
+                in1=acc[i, h, n0][:, 0 : n1 - n0],
                 op0=ALU.mult,
                 op1=ALU.add,
             )
-            nc.sync.dma_start(out=out_rows[:, i, cols], in_=t[:])
+            free_banks.append(acc_bank[i, h, n0])
+            nc.sync.dma_start(out=out_rows[:, i, cols], in_=t[:, 0 : n1 - n0])
 
         scale(0)
         turn([0])
-        interleave_c(nc.vector.tensor_copy, 0, 0, 0, HEAD_VECTOR_COLS)
-        interleave_c(nc.scalar.copy, 0, 0, HEAD_VECTOR_COLS, N_HALF)
         scale(1)
         turn([1])
         quantise_x(0)
-        quantise_c(0, 0)
+        interleave_c(nc.vector.tensor_copy, 0, 0, 0, HEAD_VECTOR_COLS)
+        multiply(0, 0, STYLED)
+        multiply(0, 1, STYLED)
+        scale(2)
         quantise_x(1)
+        interleave_c(nc.scalar.copy, 0, 0, HEAD_VECTOR_COLS, N_HALF)
+        turn([2])
+        multiply(1, 0, STYLED)
+        multiply(1, 1, STYLED)
         interleave_c(nc.vector.tensor_copy, 1, 0, 0, HEAD_VECTOR_COLS)
         interleave_c(nc.scalar.copy, 1, 0, HEAD_VECTOR_COLS, N_HALF)
-        multiply(0, 0, STYLED)
-        multiply(1, 0, STYLED)
-        scale(2)
-        spread_mean()
-        turn([2])
-        quantise_c(1, 0)
-        multiply(0, 0, KEPT)
-        multiply(1, 0, KEPT)
         scale(3)
         quantise_x(2)
+        quantise_c(0, 0)
+        turn([3])
+        multiply(2, 0, STYLED)
+        spread_mean()
+        multiply(2, 1, STYLED)
+        quantise_c(1, 0)
+        scale(4)
+        quantise_x(3)
+        multiply(0, 0, KEPT)
+        multiply(1, 0, KEPT)
+        multiply(2, 0, KEPT)
         finish(0, 0)
+        finish(1, 0)
 
         pieces = [(g, c) for g in range(PASSES) for c in range(0, N_HALF, LATE_PIECE_COLS)]
-        steps = LEAD - 2
-        for j in range(2, LEAD):
+        first_pair = EARLY + LEAD
+        steps = LEAD - 1
+        for j in range(EARLY, first_pair):
             turn([j + 1])
-            s = j - 2
+            s = j - EARLY
             mine = pieces[s * len(pieces) // steps : (s + 1) * len(pieces) // steps]
             for g, c in mine:
                 interleave_c(nc.scalar.copy, g, 1, c, c + LATE_PIECE_COLS)
@@ -246,12 +265,16 @@ def tile_whitening_colouring_blend_s1_kernel(
             for g, c in mine:
                 if c + LATE_PIECE_COLS == N_HALF:
                     quantise_c(g, 1)
-        scale(LEAD + 2)
+        for i in range(EARLY):
+            multiply(i, 1, KEPT)
+        finish(first_pair - 1, 0)
+        scale(first_pair + 2)
+        finish(0, 1)
+        finish(1, 1)
 
-        last = (LEAD - 1, 0)
-        for j in range(LEAD, TILES, 2):
-            ahead = [i for i in (j + 1, j + 2) if i < TILES]
-            turn(ahead)
+        last = (EARLY - 1, 1)
+        for j in range(first_pair, TILES - 1, 2):
+            turn([j + 1, j + 2])
             finish(*last)
             unit(j, 0)
             if j + 3 < TILES:
@@ -261,16 +284,17 @@ def tile_whitening_colouring_blend_s1_kernel(
             unit(j - LEAD, 1)
             if j + 4 < TILES:
                 scale(j + 4)
-            if j + 2 < TILES:
-                quantise_x(j + 2)
+            quantise_x(j + 2)
             unit(j + 1, 0)
             finish(j - LEAD, 1)
             unit(j + 1 - LEAD, 1)
             finish(j + 1, 0)
             last = (j + 1 - LEAD, 1)
 
-        for i in range(TILES - LEAD, TILES):
-            unit(i, 1)
+        rest = [(TILES - 1, 0, 0, N_HALF)] + [(i, 1, 0, N_HALF) for i in range(TILES - 1 - LEAD, TILES - 1)]
+        rest = rest + [(TILES - 1, 1, n0, n0 + P) for n0 in range(0, N_HALF, P)]
+        for part in rest:
+            unit(*part)
             finish(*last)
-            last = (i, 1)
+            last = part
         finish(*last)

@@ -14,6 +14,7 @@ U8 = mybir.dt.uint8
 FP8X4 = mybir.dt.float8_e4m3fn_x4
 FP4X4 = mybir.dt.float4_e2m1fn_x4
 ALU = mybir.AluOpType
+ACT = mybir.ActivationFunctionType
 
 P = 128
 PACK = 4
@@ -25,6 +26,8 @@ HALVES = N // N_HALF
 STYLED, KEPT = 0, 1
 EARLY = 3
 LEAD = 6
+FLIPPED = 4
+TURNED = TILES - FLIPPED
 HEAD_VECTOR_COLS = 320
 LATE_PIECE_COLS = 128
 
@@ -33,8 +36,12 @@ def tile_whitening_colouring_blend_s1_kernel(
     tc, x, strength, style_words, style_scales, content_root, style_mean, out
 ):
     nc = tc.nc
-    x_rows = x.rearrange("(p i) k -> p i k", i=TILES)
-    out_rows = out.rearrange("(p i) n -> p i n", i=TILES)
+    base = P * TURNED
+    x_rows = x[0:base, :].rearrange("(p i) k -> p i k", i=TURNED)
+    x_chunks = x[base:M, :].rearrange("r (g q e) -> (r g) q e", g=PASSES, q=4)
+    x_chunks = x_chunks.rearrange("(c i m) q e -> c q i m e", c=4, i=32)
+    out_turned = out[0:base, :].rearrange("(p i) n -> p i n", i=TURNED)
+    out_flipped = out[base:M, :].rearrange("(p i) n -> p i n", i=FLIPPED)
 
     with ExitStack() as ctx:
         keep = ctx.enter_context(tc.tile_pool(name="keep", bufs=1))
@@ -48,7 +55,9 @@ def tile_whitening_colouring_blend_s1_kernel(
         v_scales = keep.tile([P, PASSES, N], U8, name="v_scales", align_bytes=64)
         nc.vector.memset(v_scales[:].rearrange("p g n -> p (g n)").bitcast(I32), 0)
 
-        a_bf = keep.tile([P, TILES], BF16, name="a_bf")
+        a_bf = keep.tile([P, TURNED], BF16, name="a_bf")
+        a_quad = keep.tile([P, 4, FLIPPED], BF16, name="a_quad")
+        x_quad = {}
         mean_part = keep.tile([P, N // P], BF16, name="mean_part")
         x_sb = {}
         c_raw = {}
@@ -73,7 +82,7 @@ def tile_whitening_colouring_blend_s1_kernel(
             nc.sync.dma_start(out=t[:].bitcast(I32), in_=src.rearrange("g p w -> p g w"))
             v_words[h] = t
 
-        nc.sync.dma_start(out=a_bf[:], in_=strength.rearrange("(p i) -> p i", i=TILES))
+        nc.sync.dma_start(out=a_bf[:], in_=strength[0:base].rearrange("(p i) -> p i", i=TURNED))
         load_x(0, 1)
         load_x(1, 1)
         load_v(0)
@@ -91,14 +100,30 @@ def tile_whitening_colouring_blend_s1_kernel(
         load_x(5, 1)
         load_c(1, 1)
         load_x(6, 2)
-        for first in range(8, TILES, 4):
-            load_x(first, 4)
+        for q in range(4):
+            nc.sync.dma_start(
+                out=a_quad[32 * q : 32 * q + 32, :, :], in_=strength[base:M].rearrange("(c i t) -> i c t", c=4, i=32)
+            )
+        load_x(8, TURNED - 8)
+        for c in range(4):
+            x_quad[c] = keep.tile([P, FLIPPED * PASSES * P], BF16, name="x_quad_%d" % c)
+            for q in range(4):
+                nc.sync.dma_start(out=x_quad[c][32 * q : 32 * q + 32, :].rearrange("i (m e) -> i m e", e=P), in_=x_chunks[c, q])
 
-        share = keep.tile([P, 2, TILES], F32, name="share")
-        nc.vector.tensor_copy(out=share[:, STYLED, :], in_=a_bf[:])
-        nc.vector.tensor_scalar(
-            out=share[:, KEPT, :], in0=a_bf[:], scalar1=-1.0, scalar2=1.0, op0=ALU.mult, op1=ALU.add
-        )
+        share = keep.tile([P, 2, TURNED], F32, name="share")
+        share_late = keep.tile([P, FLIPPED], F32, name="share_late")
+        share_quad = keep.tile([P, 2, 4 * FLIPPED], F32, name="share_quad")
+
+        def make_shares(dst, src):
+            nc.vector.tensor_copy(out=dst[:, STYLED, :], in_=src)
+            nc.vector.tensor_scalar(out=dst[:, KEPT, :], in0=src, scalar1=-1.0, scalar2=1.0, op0=ALU.mult, op1=ALU.add)
+
+        make_shares(share, a_bf[:])
+
+        def make_late_shares():
+            for c in range(4):
+                nc.vector.tensor_copy(out=share_late[32 * c : 32 * c + 32, :], in_=a_quad[32 * c : 32 * c + 32, c, :])
+            make_shares(share_quad, a_quad[:].rearrange("p c t -> p (c t)"))
 
         mean_all = keep.tile([P, N], BF16, name="mean_all")
         c_grouped = {}
@@ -175,6 +200,32 @@ def tile_whitening_colouring_blend_s1_kernel(
                     free_banks.append(banks[i, o][0])
                 turned[i] = t
 
+        flipped = {}
+
+        def scale_quad(i):
+            t = i - TURNED
+            dst = stage.tile([P, 2 * K], BF16, name="scaled_quad", tag="scaled_quad", bufs=2, align_bytes=64)
+            parts = dst[:].rearrange("p (c u o w e) -> p c o u w e", c=4, u=2, o=2, e=2)
+            for c in range(4):
+                src = x_quad[c][:, PASSES * P * t : PASSES * P * (t + 1)].rearrange("p (w u e) -> p u w e", u=2, e=2)
+                for o in (STYLED, KEPT):
+                    col = c * FLIPPED + t
+                    nc.scalar.activation(out=parts[:, c, o], in_=src, func=ACT.Copy, scale=share_quad[:, o, col : col + 1])
+            scaled[i] = dst
+
+        def flip(i):
+            dst = stage.tile([P, K], F32, name="flipped", tag="flipped", bufs=2, align_bytes=64)
+            nc.vector.transpose(out=dst[:], in_=scaled[i][:].bitcast(F32))
+            flipped[i] = dst
+
+        def regroup(i):
+            dst = stage.tile([P, 2 * K], BF16, name="turned", tag="turned", align_bytes=64)
+            nc.scalar.copy(
+                out=dst[:].bitcast(F32).rearrange("p (v c i u) -> p v c i u", v=4, c=4, u=2),
+                in_=flipped[i][:].rearrange("p (c u v i) -> p v c i u", c=4, u=2, v=4),
+            )
+            turned[i] = dst
+
         def quantise_x(i):
             nc.vector.quantize_mx(out=x_codes[i][:].bitcast(FP8X4), scales=x_scales[i][:], in_=turned[i][:])
 
@@ -209,13 +260,14 @@ def tile_whitening_colouring_blend_s1_kernel(
             nc.vector.scalar_tensor_tensor(
                 out=t[:, 0 : n1 - n0],
                 in0=mean_all[:, cols],
-                scalar=share[:, STYLED, i : i + 1],
+                scalar=share[:, STYLED, i : i + 1] if i < TURNED else share_late[:, i - TURNED : i - TURNED + 1],
                 in1=acc[i, h, n0][:, 0 : n1 - n0],
                 op0=ALU.mult,
                 op1=ALU.add,
             )
             free_banks.append(acc_bank[i, h, n0])
-            nc.sync.dma_start(out=out_rows[:, i, cols], in_=t[:, 0 : n1 - n0])
+            rows = out_turned[:, i, cols] if i < TURNED else out_flipped[:, i - TURNED, cols]
+            nc.sync.dma_start(out=rows, in_=t[:, 0 : n1 - n0])
 
         scale(0)
         turn([0])
@@ -260,41 +312,42 @@ def tile_whitening_colouring_blend_s1_kernel(
                 interleave_c(nc.scalar.copy, g, 1, c, c + LATE_PIECE_COLS)
             finish(j - 1, 0)
             unit(j, 0)
-            scale(j + 2)
+            if j + 2 < TURNED:
+                scale(j + 2)
             quantise_x(j + 1)
             for g, c in mine:
                 if c + LATE_PIECE_COLS == N_HALF:
                     quantise_c(g, 1)
+            if j == first_pair - 2:
+                make_late_shares()
+        scale_quad(TURNED)
         for i in range(EARLY):
             multiply(i, 1, KEPT)
         finish(first_pair - 1, 0)
-        scale(first_pair + 2)
+        pair = list(range(first_pair + 1, TURNED))
+        if pair:
+            scale(first_pair + 2)
         finish(0, 1)
         finish(1, 1)
+        if pair:
+            turn(pair)
 
+        todo = [(first_pair, 0, 0, N_HALF)] + [(i, 1, 0, N_HALF) for i in range(EARLY, first_pair + 1)]
+        todo = todo + [(i, h, 0, N_HALF) for i in range(first_pair + 1, TILES) for h in range(HALVES)]
+        todo = todo[:-1] + [(TILES - 1, 1, n0, n0 + P) for n0 in range(0, N_HALF, P)]
         last = (EARLY - 1, 1)
-        for j in range(first_pair, TILES - 1, 2):
-            turn([j + 1, j + 2])
-            finish(*last)
-            unit(j, 0)
-            if j + 3 < TILES:
-                scale(j + 3)
-            quantise_x(j + 1)
-            finish(j, 0)
-            unit(j - LEAD, 1)
-            if j + 4 < TILES:
-                scale(j + 4)
-            quantise_x(j + 2)
-            unit(j + 1, 0)
-            finish(j - LEAD, 1)
-            unit(j + 1 - LEAD, 1)
-            finish(j + 1, 0)
-            last = (j + 1 - LEAD, 1)
-
-        rest = [(TILES - 1, 0, 0, N_HALF)] + [(i, 1, 0, N_HALF) for i in range(TILES - 1 - LEAD, TILES - 1)]
-        rest = rest + [(TILES - 1, 1, n0, n0 + P) for n0 in range(0, N_HALF, P)]
-        for part in rest:
+        for n, part in enumerate(todo):
+            i = TURNED + n // 3
+            if n % 3 == 0 and i < TILES:
+                flip(i)
+                if i + 1 < TILES:
+                    scale_quad(i + 1)
+                regroup(i)
+            if n % 3 == 0 and TURNED < i <= TILES:
+                quantise_x(i - 1)
             unit(*part)
             finish(*last)
             last = part
+            if n < len(pair):
+                quantise_x(pair[n])
         finish(*last)

@@ -24,10 +24,13 @@ TILES = M // P
 N_HALF = 512
 HALVES = N // N_HALF
 STYLED, KEPT = 0, 1
+BOTH = (STYLED, KEPT)
 EARLY = 3
 LEAD = 6
 FLIPPED = 4
 TURNED = TILES - FLIPPED
+FLIP_START = 4
+FLIP_PERIOD = 3
 HEAD_VECTOR_COLS = 320
 LATE_PIECE_COLS = 128
 
@@ -107,7 +110,7 @@ def tile_whitening_colouring_blend_s1_kernel(
         load_x(8, TURNED - 8)
         for c in range(4):
             x_quad[c] = keep.tile([P, FLIPPED * PASSES * P], BF16, name="x_quad_%d" % c)
-            for q in range(4):
+            for q in (0, 2, 1, 3):
                 nc.sync.dma_start(out=x_quad[c][32 * q : 32 * q + 32, :].rearrange("i (m e) -> i m e", e=P), in_=x_chunks[c, q])
 
         share = keep.tile([P, 2, TURNED], F32, name="share")
@@ -144,6 +147,7 @@ def tile_whitening_colouring_blend_s1_kernel(
         turned = {}
         acc = {}
         acc_bank = {}
+        banks = {}
         free_banks = list(range(8))
 
         def take_bank():
@@ -155,6 +159,10 @@ def tile_whitening_colouring_blend_s1_kernel(
             words = mean_part[:].bitcast(F32)
             for c in range(4):
                 nc.tensor.transpose(bank[:, c * P : (c + 1) * P], words[:, c : c + 1].to_broadcast([P, P]), ident[:])
+            banks["mean"] = (b, bank)
+
+        def collect_mean():
+            b, bank = banks["mean"]
             nc.scalar.copy(
                 out=mean_all[:].bitcast(F32).rearrange("p (j c) -> p j c", c=4),
                 in_=bank[:].rearrange("p (c j) -> p j c", c=4),
@@ -169,8 +177,8 @@ def tile_whitening_colouring_blend_s1_kernel(
         def quantise_c(g, h):
             nc.vector.quantize_mx(out=c_codes[g, h][:].bitcast(FP8X4), scales=c_scales[g, h][:], in_=c_grouped[g, h][:])
 
-        def scale(i):
-            for o in (STYLED, KEPT):
+        def scale(i, operands=BOTH):
+            for o in operands:
                 t = stage.tile([P, K], BF16, name="scaled", tag="scaled%d" % o)
                 nc.vector.tensor_scalar(
                     out=t[:].rearrange("p (u w e) -> p u w e", u=2, e=2),
@@ -181,24 +189,27 @@ def tile_whitening_colouring_blend_s1_kernel(
                 )
                 scaled[i, o] = t
 
-        def turn(tiles):
-            banks = {}
-            for i in tiles:
-                for o in (STYLED, KEPT):
-                    b, bank = take_bank()
-                    words = scaled[i, o][:].bitcast(F32)
-                    for s in range(4):
-                        nc.tensor.transpose(bank[:, s * P : (s + 1) * P], words[:, s * P : (s + 1) * P], ident[:])
-                    banks[i, o] = (b, bank)
-            for i in tiles:
-                t = stage.tile([P, 2 * K], BF16, name="turned", tag="turned", align_bytes=64)
-                for o in (STYLED, KEPT):
-                    nc.scalar.copy(
-                        out=t[:, o * K : (o + 1) * K].bitcast(F32).rearrange("p (g r u) -> p g r u", g=PASSES, u=2),
-                        in_=banks[i, o][1][:].rearrange("p (u g r) -> p g r u", u=2, g=PASSES),
-                    )
-                    free_banks.append(banks[i, o][0])
-                turned[i] = t
+        def turn(parts):
+            for i, o in parts:
+                b, bank = take_bank()
+                words = scaled[i, o][:].bitcast(F32)
+                for s in range(4):
+                    nc.tensor.transpose(bank[:, s * P : (s + 1) * P], words[:, s * P : (s + 1) * P], ident[:])
+                banks[i, o] = (b, bank)
+
+        def collect(parts):
+            for i, o in parts:
+                if i not in turned:
+                    turned[i] = stage.tile([P, 2 * K], BF16, name="turned", tag="turned", align_bytes=64)
+                b, bank = banks[i, o]
+                nc.scalar.copy(
+                    out=turned[i][:, o * K : (o + 1) * K].bitcast(F32).rearrange("p (g r u) -> p g r u", g=PASSES, u=2),
+                    in_=bank[:].rearrange("p (u g r) -> p g r u", u=2, g=PASSES),
+                )
+                free_banks.append(b)
+
+        def whole(tiles):
+            return [(i, o) for i in tiles for o in BOTH]
 
         flipped = {}
 
@@ -226,8 +237,12 @@ def tile_whitening_colouring_blend_s1_kernel(
             )
             turned[i] = dst
 
-        def quantise_x(i):
-            nc.vector.quantize_mx(out=x_codes[i][:].bitcast(FP8X4), scales=x_scales[i][:], in_=turned[i][:])
+        def quantise_x(i, operands=BOTH):
+            first, last = operands[0], operands[-1] + 1
+            cols = slice(first * PASSES * P, last * PASSES * P)
+            nc.vector.quantize_mx(
+                out=x_codes[i][:, cols].bitcast(FP8X4), scales=x_scales[i][:, cols], in_=turned[i][:, first * K : last * K]
+            )
 
         def multiply(i, h, o, n0=0, n1=N_HALF):
             if o == STYLED:
@@ -256,7 +271,7 @@ def tile_whitening_colouring_blend_s1_kernel(
 
         def finish(i, h, n0=0, n1=N_HALF):
             cols = slice(h * N_HALF + n0, h * N_HALF + n1)
-            t = stage.tile([P, N_HALF], F32, name="result", tag="result", bufs=8)
+            t = stage.tile([P, N_HALF], F32, name="result", tag="result", bufs=16)
             nc.vector.scalar_tensor_tensor(
                 out=t[:, 0 : n1 - n0],
                 in0=mean_all[:, cols],
@@ -269,81 +284,99 @@ def tile_whitening_colouring_blend_s1_kernel(
             rows = out_turned[:, i, cols] if i < TURNED else out_flipped[:, i - TURNED, cols]
             nc.sync.dma_start(out=rows, in_=t[:, 0 : n1 - n0])
 
-        scale(0)
-        turn([0])
-        scale(1)
-        turn([1])
-        quantise_x(0)
-        interleave_c(nc.vector.tensor_copy, 0, 0, 0, HEAD_VECTOR_COLS)
+        pieces = [(g, c) for g in range(PASSES) for c in range(0, N_HALF, LATE_PIECE_COLS)]
+
+        def interleave_late(count):
+            done = []
+            for n in range(min(count, len(pieces))):
+                g, c = pieces.pop(0)
+                interleave_c(nc.scalar.copy, g, 1, c, c + LATE_PIECE_COLS)
+                if c + LATE_PIECE_COLS == N_HALF:
+                    done.append(g)
+            return done
+
+        S, Kp = (STYLED,), (KEPT,)
+        scale(0, S)
+        scale(1, S)
+        scale(0, Kp)
+        scale(1, Kp)
+        turn([(0, STYLED), (1, STYLED), (0, KEPT)])
+        collect([(0, STYLED), (1, STYLED)])
+        quantise_x(0, S)
+        quantise_x(1, S)
+        collect([(0, KEPT)])
         multiply(0, 0, STYLED)
-        multiply(0, 1, STYLED)
-        scale(2)
-        quantise_x(1)
-        interleave_c(nc.scalar.copy, 0, 0, HEAD_VECTOR_COLS, N_HALF)
-        turn([2])
         multiply(1, 0, STYLED)
-        multiply(1, 1, STYLED)
-        interleave_c(nc.vector.tensor_copy, 1, 0, 0, HEAD_VECTOR_COLS)
-        interleave_c(nc.scalar.copy, 1, 0, HEAD_VECTOR_COLS, N_HALF)
-        scale(3)
-        quantise_x(2)
-        quantise_c(0, 0)
-        turn([3])
-        multiply(2, 0, STYLED)
+        interleave_c(nc.vector.tensor_copy, 0, 0, 0, HEAD_VECTOR_COLS)
+        interleave_c(nc.scalar.copy, 0, 0, HEAD_VECTOR_COLS, N_HALF)
+        scale(2)
+        turn([(2, STYLED), (1, KEPT), (2, KEPT)])
         spread_mean()
+        collect([(2, STYLED)])
+        multiply(0, 1, STYLED)
+        multiply(1, 1, STYLED)
+        quantise_c(0, 0)
+        interleave_c(nc.vector.tensor_copy, 1, 0, 0, HEAD_VECTOR_COLS)
+        quantise_x(2, S)
+        interleave_c(nc.scalar.copy, 1, 0, HEAD_VECTOR_COLS, N_HALF)
+        collect([(1, KEPT), (2, KEPT)])
+        collect_mean()
+        scale(3)
+        multiply(2, 0, STYLED)
         multiply(2, 1, STYLED)
+        quantise_x(0, Kp)
         quantise_c(1, 0)
+        quantise_x(1, Kp)
+        interleave_late(1)
+        turn(whole([3]))
+        collect(whole([3]))
+        interleave_late(2)
+        quantise_x(2, Kp)
         scale(4)
-        quantise_x(3)
         multiply(0, 0, KEPT)
         multiply(1, 0, KEPT)
         multiply(2, 0, KEPT)
         finish(0, 0)
+        quantise_x(3)
         finish(1, 0)
 
-        pieces = [(g, c) for g in range(PASSES) for c in range(0, N_HALF, LATE_PIECE_COLS)]
         first_pair = EARLY + LEAD
-        steps = LEAD - 1
         for j in range(EARLY, first_pair):
-            turn([j + 1])
-            s = j - EARLY
-            mine = pieces[s * len(pieces) // steps : (s + 1) * len(pieces) // steps]
-            for g, c in mine:
-                interleave_c(nc.scalar.copy, g, 1, c, c + LATE_PIECE_COLS)
+            turn(whole([j + 1]))
+            collect(whole([j + 1]))
+            done = interleave_late(1)
             finish(j - 1, 0)
             unit(j, 0)
-            if j + 2 < TURNED:
-                scale(j + 2)
+            scale(j + 2)
             quantise_x(j + 1)
-            for g, c in mine:
-                if c + LATE_PIECE_COLS == N_HALF:
-                    quantise_c(g, 1)
-            if j == first_pair - 2:
+            for g in done:
+                quantise_c(g, 1)
+            if j == first_pair - 3:
                 make_late_shares()
-        scale_quad(TURNED)
         for i in range(EARLY):
             multiply(i, 1, KEPT)
         finish(first_pair - 1, 0)
         pair = list(range(first_pair + 1, TURNED))
-        if pair:
-            scale(first_pair + 2)
+        scale(first_pair + 2)
         finish(0, 1)
         finish(1, 1)
-        if pair:
-            turn(pair)
+        turn(whole(pair))
+        collect(whole(pair))
+        scale_quad(TURNED)
 
         todo = [(first_pair, 0, 0, N_HALF)] + [(i, 1, 0, N_HALF) for i in range(EARLY, first_pair + 1)]
         todo = todo + [(i, h, 0, N_HALF) for i in range(first_pair + 1, TILES) for h in range(HALVES)]
         todo = todo[:-1] + [(TILES - 1, 1, n0, n0 + P) for n0 in range(0, N_HALF, P)]
         last = (EARLY - 1, 1)
         for n, part in enumerate(todo):
-            i = TURNED + n // 3
-            if n % 3 == 0 and i < TILES:
+            step, phase = divmod(n - FLIP_START, FLIP_PERIOD)
+            i = TURNED + step
+            if phase == 0 and TURNED <= i < TILES:
                 flip(i)
                 if i + 1 < TILES:
                     scale_quad(i + 1)
                 regroup(i)
-            if n % 3 == 0 and TURNED < i <= TILES:
+            if phase == 0 and TURNED < i <= TILES:
                 quantise_x(i - 1)
             unit(*part)
             finish(*last)

@@ -30,6 +30,8 @@ LEAD = 6
 FLIPPED = 4
 TURNED = TILES - FLIPPED
 FLIP_START = 4
+WARM_FIRST = 15
+WARM_SECOND = 8
 FLIP_PERIOD = 3
 HEAD_VECTOR_COLS = 320
 LATE_PIECE_COLS = 128
@@ -54,6 +56,12 @@ def tile_whitening_colouring_blend_s1_kernel(
 
         ident = keep.tile([P, P], F32, name="ident")
         make_identity(nc, ident[:])
+
+        warm_in = keep.tile([P, K_PASS], BF16, name="warm_in", align_bytes=64)
+        warm_codes = keep.tile([P, P], U32, name="warm_codes", align_bytes=64)
+        warm_scales = keep.tile([P, P], U8, name="warm_scales", align_bytes=64)
+        nc.vector.memset(warm_in[:], 0.0)
+        nc.vector.quantize_mx(out=warm_codes[:].bitcast(FP8X4), scales=warm_scales[:], in_=warm_in[:])
 
         v_scales = keep.tile([P, PASSES, N], U8, name="v_scales", align_bytes=64)
         nc.vector.memset(v_scales[:].rearrange("p g n -> p (g n)").bitcast(I32), 0)
@@ -92,10 +100,10 @@ def tile_whitening_colouring_blend_s1_kernel(
         for q in range(4):
             src = style_scales.bitcast(I32)[:, 4 * q : 4 * q + 4, :]
             nc.sync.dma_start(out=v_scales[32 * q : 32 * q + 4, :, :].bitcast(I32), in_=src.rearrange("g r w -> r g w"))
-        nc.sync.dma_start(out=mean_part[:], in_=style_mean.rearrange("(p c) -> p c", p=P))
-        load_c(0, 0)
-        load_v(1)
         load_x(2, 1)
+        load_c(0, 0)
+        nc.sync.dma_start(out=mean_part[:], in_=style_mean.rearrange("(p c) -> p c", p=P))
+        load_v(1)
         load_c(1, 0)
         load_x(3, 1)
         load_x(4, 1)
@@ -103,11 +111,11 @@ def tile_whitening_colouring_blend_s1_kernel(
         load_x(5, 1)
         load_c(1, 1)
         load_x(6, 2)
+        load_x(8, 4)
         for q in range(4):
             nc.sync.dma_start(
                 out=a_quad[32 * q : 32 * q + 32, :, :], in_=strength[base:M].rearrange("(c i t) -> i c t", c=4, i=32)
             )
-        load_x(8, TURNED - 8)
         for c in range(4):
             x_quad[c] = keep.tile([P, FLIPPED * PASSES * P], BF16, name="x_quad_%d" % c)
             for q in (0, 2, 1, 3):
@@ -125,8 +133,10 @@ def tile_whitening_colouring_blend_s1_kernel(
 
         def make_late_shares():
             for c in range(4):
-                nc.vector.tensor_copy(out=share_late[32 * c : 32 * c + 32, :], in_=a_quad[32 * c : 32 * c + 32, c, :])
-            make_shares(share_quad, a_quad[:].rearrange("p c t -> p (c t)"))
+                nc.scalar.copy(out=share_late[32 * c : 32 * c + 32, :], in_=a_quad[32 * c : 32 * c + 32, c, :])
+            src = a_quad[:].rearrange("p c t -> p (c t)")
+            nc.scalar.copy(out=share_quad[:, STYLED, :], in_=src)
+            nc.scalar.activation(out=share_quad[:, KEPT, :], in_=src, func=ACT.Copy, scale=-1.0, bias=1.0)
 
         mean_all = keep.tile([P, N], BF16, name="mean_all")
         c_grouped = {}
@@ -153,6 +163,21 @@ def tile_whitening_colouring_blend_s1_kernel(
         def take_bank():
             b = free_banks.pop(0)
             return b, psum.tile([P, N_HALF], F32, name="bank", tag="bank%d" % b)
+
+        def warm_up(count):
+            b, bank = take_bank()
+            for n in range(count):
+                cols = slice((n % 4) * P, (n % 4 + 1) * P)
+                nc.tensor.matmul_mx(
+                    out=bank[:, cols],
+                    lhsT=warm_codes[:].bitcast(FP8X4),
+                    lhsT_scale=warm_scales[:],
+                    rhs=warm_codes[:].bitcast(FP8X4),
+                    rhs_scale=warm_scales[:],
+                    start=True,
+                    stop=True,
+                )
+            free_banks.append(b)
 
         def spread_mean():
             b, bank = take_bank()
@@ -296,41 +321,45 @@ def tile_whitening_colouring_blend_s1_kernel(
             return done
 
         S, Kp = (STYLED,), (KEPT,)
+        warm_up(WARM_FIRST)
         scale(0, S)
         scale(1, S)
         scale(0, Kp)
         scale(1, Kp)
-        turn([(0, STYLED), (1, STYLED), (0, KEPT)])
-        collect([(0, STYLED), (1, STYLED)])
+        turn([(0, STYLED)])
+        collect([(0, STYLED)])
+        warm_up(WARM_SECOND)
+        turn([(1, STYLED), (0, KEPT)])
+        collect([(1, STYLED)])
         quantise_x(0, S)
+        scale(2)
         quantise_x(1, S)
         collect([(0, KEPT)])
         multiply(0, 0, STYLED)
-        multiply(1, 0, STYLED)
         interleave_c(nc.vector.tensor_copy, 0, 0, 0, HEAD_VECTOR_COLS)
         interleave_c(nc.scalar.copy, 0, 0, HEAD_VECTOR_COLS, N_HALF)
-        scale(2)
         turn([(2, STYLED), (1, KEPT), (2, KEPT)])
         spread_mean()
         collect([(2, STYLED)])
+        multiply(1, 0, STYLED)
         multiply(0, 1, STYLED)
         multiply(1, 1, STYLED)
         quantise_c(0, 0)
-        interleave_c(nc.vector.tensor_copy, 1, 0, 0, HEAD_VECTOR_COLS)
         quantise_x(2, S)
+        collect([(1, KEPT)])
+        interleave_c(nc.vector.tensor_copy, 1, 0, 0, HEAD_VECTOR_COLS)
         interleave_c(nc.scalar.copy, 1, 0, HEAD_VECTOR_COLS, N_HALF)
-        collect([(1, KEPT), (2, KEPT)])
-        collect_mean()
         scale(3)
         multiply(2, 0, STYLED)
         multiply(2, 1, STYLED)
         quantise_x(0, Kp)
         quantise_c(1, 0)
         quantise_x(1, Kp)
-        interleave_late(1)
+        collect([(2, KEPT)])
+        collect_mean()
         turn(whole([3]))
         collect(whole([3]))
-        interleave_late(2)
+        interleave_late(3)
         quantise_x(2, Kp)
         scale(4)
         multiply(0, 0, KEPT)
@@ -344,15 +373,13 @@ def tile_whitening_colouring_blend_s1_kernel(
         for j in range(EARLY, first_pair):
             turn(whole([j + 1]))
             collect(whole([j + 1]))
-            done = interleave_late(1)
+            interleave_late(1)
             finish(j - 1, 0)
             unit(j, 0)
             scale(j + 2)
             quantise_x(j + 1)
-            for g in done:
-                quantise_c(g, 1)
-            if j == first_pair - 3:
-                make_late_shares()
+            if j - EARLY in (1, 4):
+                quantise_c((1, 4).index(j - EARLY), 1)
         for i in range(EARLY):
             multiply(i, 1, KEPT)
         finish(first_pair - 1, 0)
@@ -362,6 +389,7 @@ def tile_whitening_colouring_blend_s1_kernel(
         finish(1, 1)
         turn(whole(pair))
         collect(whole(pair))
+        make_late_shares()
         scale_quad(TURNED)
 
         todo = [(first_pair, 0, 0, N_HALF)] + [(i, 1, 0, N_HALF) for i in range(EARLY, first_pair + 1)]

from contextlib import ExitStack

import concourse.mybir as mybir
from concourse.masks import make_identity

M, K, N = 2048, 1024, 1024
FLOPS = 2 * 2 * M * K * N

F32 = mybir.dt.float32
BF16 = mybir.dt.bfloat16
I32 = mybir.dt.int32
U32 = mybir.dt.uint32
U8 = mybir.dt.uint8
FP8X4 = mybir.dt.float8_e4m3fn_x4
FP4X4 = mybir.dt.float4_e2m1fn_x4
ALU = mybir.AluOpType
ACT = mybir.ActivationFunctionType

P = 128
PACK = 4
K_PASS = P * PACK
PASSES = K // K_PASS
TILES = M // P
N_HALF = 512
HALVES = N // N_HALF
STYLED, KEPT = 0, 1
BOTH = (STYLED, KEPT)
EARLY = 3
LEAD = 6
FLIPPED = 4
TURNED = TILES - FLIPPED
FLIP_START = 4
WARM_FIRST = 15
WARM_SECOND = 8
FLIP_PERIOD = 3
HEAD_VECTOR_COLS = 320
LATE_PIECE_COLS = 128


def tile_whitening_colouring_blend_s1_kernel(
    tc, x, strength, style_words, style_scales, content_root, style_mean, out
):
    nc = tc.nc
    base = P * TURNED
    x_rows = x[0:base, :].rearrange("(p i) k -> p i k", i=TURNED)
    x_chunks = x[base:M, :].rearrange("r (g q e) -> (r g) q e", g=PASSES, q=4)
    x_chunks = x_chunks.rearrange("(c i m) q e -> c q i m e", c=4, i=32)
    out_turned = out[0:base, :].rearrange("(p i) n -> p i n", i=TURNED)
    out_flipped = out[base:M, :].rearrange("(p i) n -> p i n", i=FLIPPED)

    with ExitStack() as ctx:
        keep = ctx.enter_context(tc.tile_pool(name="keep", bufs=1))
        stage = ctx.enter_context(tc.tile_pool(name="stage", bufs=4))
        psum = ctx.enter_context(tc.psum_pool(name="psum", bufs=1))
        ctx.enter_context(tc.manual_schedule())

        ident = keep.tile([P, P], F32, name="ident")
        make_identity(nc, ident[:])

        warm_in = keep.tile([P, K_PASS], BF16, name="warm_in", align_bytes=64)
        warm_codes = keep.tile([P, P], U32, name="warm_codes", align_bytes=64)
        warm_scales = keep.tile([P, P], U8, name="warm_scales", align_bytes=64)
        nc.vector.memset(warm_in[:], 0.0)
        nc.vector.quantize_mx(out=warm_codes[:].bitcast(FP8X4), scales=warm_scales[:], in_=warm_in[:])

        v_scales = keep.tile([P, PASSES, N], U8, name="v_scales", align_bytes=64)
        nc.vector.memset(v_scales[:].rearrange("p g n -> p (g n)").bitcast(I32), 0)

        a_bf = keep.tile([P, TURNED], BF16, name="a_bf")
        a_quad = keep.tile([P, 4, FLIPPED], BF16, name="a_quad")
        x_quad = {}
        mean_part = keep.tile([P, N // P], BF16, name="mean_part")
        x_sb = {}
        c_raw = {}
        v_words = {}

        def load_x(first, count):
            t = keep.tile([P, count * K], BF16, name="x_%d" % first)
            nc.sync.dma_start(out=t[:], in_=x_rows[:, first : first + count, :].rearrange("p i k -> p (i k)"))
            for i in range(count):
                x_sb[first + i] = t[:, i * K : (i + 1) * K]

        def load_c(g, h):
            t = keep.tile([P, PACK, N_HALF], BF16, name="c_raw_%d_%d" % (g, h))
            rows = content_root[g * K_PASS : (g + 1) * K_PASS, h * N_HALF : (h + 1) * N_HALF]
            nc.sync.dma_start(out=t[:], in_=rows.rearrange("(p t) n -> p t n", t=PACK))
            c_raw[g, h] = t

        def load_v(h):
            t = keep.tile([P, PASSES, 2 * N_HALF], U8, name="v_words_%d" % h, align_bytes=64)
            width = N_HALF // 2
            src = style_words.bitcast(I32)[:, :, h * width : (h + 1) * width]
            nc.sync.dma_start(out=t[:].bitcast(I32), in_=src.rearrange("g p w -> p g w"))
            v_words[h] = t

        nc.sync.dma_start(out=a_bf[:], in_=strength[0:base].rearrange("(p i) -> p i", i=TURNED))
        load_x(0, 1)
        load_x(1, 1)
        load_v(0)
        for q in range(4):
            src = style_scales.bitcast(I32)[:, 4 * q : 4 * q + 4, :]
            nc.sync.dma_start(out=v_scales[32 * q : 32 * q + 4, :, :].bitcast(I32), in_=src.rearrange("g r w -> r g w"))
        load_x(2, 1)
        load_c(0, 0)
        nc.sync.dma_start(out=mean_part[:], in_=style_mean.rearrange("(p c) -> p c", p=P))
        load_v(1)
        load_c(1, 0)
        load_x(3, 1)
        load_x(4, 1)
        load_c(0, 1)
        load_x(5, 1)
        load_c(1, 1)
        load_x(6, 2)
        load_x(8, 4)
        for q in range(4):
            nc.sync.dma_start(
                out=a_quad[32 * q : 32 * q + 32, :, :], in_=strength[base:M].rearrange("(c i t) -> i c t", c=4, i=32)
            )
        for c in range(4):
            x_quad[c] = keep.tile([P, FLIPPED * PASSES * P], BF16, name="x_quad_%d" % c)
            for q in (0, 2, 1, 3):
                nc.sync.dma_start(out=x_quad[c][32 * q : 32 * q + 32, :].rearrange("i (m e) -> i m e", e=P), in_=x_chunks[c, q])

        share = keep.tile([P, 2, TURNED], F32, name="share")
        share_late = keep.tile([P, FLIPPED], F32, name="share_late")
        share_quad = keep.tile([P, 2, 4 * FLIPPED], F32, name="share_quad")

        def make_shares(dst, src):
            nc.vector.tensor_copy(out=dst[:, STYLED, :], in_=src)
            nc.vector.tensor_scalar(out=dst[:, KEPT, :], in0=src, scalar1=-1.0, scalar2=1.0, op0=ALU.mult, op1=ALU.add)

        make_shares(share, a_bf[:])

        def make_late_shares():
            for c in range(4):
                nc.scalar.copy(out=share_late[32 * c : 32 * c + 32, :], in_=a_quad[32 * c : 32 * c + 32, c, :])
            src = a_quad[:].rearrange("p c t -> p (c t)")
            nc.scalar.copy(out=share_quad[:, STYLED, :], in_=src)
            nc.scalar.activation(out=share_quad[:, KEPT, :], in_=src, func=ACT.Copy, scale=-1.0, bias=1.0)

        mean_all = keep.tile([P, N], BF16, name="mean_all")
        c_grouped = {}
        c_codes = {}
        c_scales = {}
        for g in range(PASSES):
            for h in range(HALVES):
                c_grouped[g, h] = keep.tile([P, N_HALF * PACK], BF16, name="c_grouped_%d_%d" % (g, h), align_bytes=64)
                c_codes[g, h] = keep.tile([P, N_HALF], U32, name="c_codes_%d_%d" % (g, h), align_bytes=64)
                c_scales[g, h] = keep.tile([P, N_HALF], U8, name="c_scales_%d_%d" % (g, h), align_bytes=64)
        x_codes = {}
        x_scales = {}
        for i in range(TILES):
            x_codes[i] = keep.tile([P, 2 * PASSES * P], U32, name="x_codes_%d" % i, align_bytes=64)
            x_scales[i] = keep.tile([P, 2 * PASSES * P], U8, name="x_scales_%d" % i, align_bytes=64)

        scaled = {}
        turned = {}
        acc = {}
        acc_bank = {}
        banks = {}
        free_banks = list(range(8))

        def take_bank():
            b = free_banks.pop(0)
            return b, psum.tile([P, N_HALF], F32, name="bank", tag="bank%d" % b)

        def warm_up(count):
            b, bank = take_bank()
            for n in range(count):
                cols = slice((n % 4) * P, (n % 4 + 1) * P)
                nc.tensor.matmul_mx(
                    out=bank[:, cols],
                    lhsT=warm_codes[:].bitcast(FP8X4),
                    lhsT_scale=warm_scales[:],
                    rhs=warm_codes[:].bitcast(FP8X4),
                    rhs_scale=warm_scales[:],
                    start=True,
                    stop=True,
                )
            free_banks.append(b)

        def spread_mean():
            b, bank = take_bank()
            words = mean_part[:].bitcast(F32)
            for c in range(4):
                nc.tensor.transpose(bank[:, c * P : (c + 1) * P], words[:, c : c + 1].to_broadcast([P, P]), ident[:])
            banks["mean"] = (b, bank)

        def collect_mean():
            b, bank = banks["mean"]
            nc.scalar.copy(
                out=mean_all[:].bitcast(F32).rearrange("p (j c) -> p j c", c=4),
                in_=bank[:].rearrange("p (c j) -> p j c", c=4),
            )
            free_banks.append(b)

        def interleave_c(engine_copy, g, h, col0, col1):
            dst = c_grouped[g, h][:, col0 * PACK : col1 * PACK].rearrange("p (c i t) -> p c t i", i=4, t=PACK)
            src = c_raw[g, h][:, :, col0:col1].rearrange("p t (c i) -> p c t i", i=4)
            engine_copy(out=dst, in_=src)

        def quantise_c(g, h):
            nc.vector.quantize_mx(out=c_codes[g, h][:].bitcast(FP8X4), scales=c_scales[g, h][:], in_=c_grouped[g, h][:])

        def scale(i, operands=BOTH):
            for o in operands:
                t = stage.tile([P, K], BF16, name="scaled", tag="scaled%d" % o)
                nc.vector.tensor_scalar(
                    out=t[:].rearrange("p (u w e) -> p u w e", u=2, e=2),
                    in0=x_sb[i].rearrange("p (w u e) -> p u w e", u=2, e=2),
                    scalar1=share[:, o, i : i + 1],
                    scalar2=None,
                    op0=ALU.mult,
                )
                scaled[i, o] = t

        def turn(parts):
            for i, o in parts:
                b, bank = take_bank()
                words = scaled[i, o][:].bitcast(F32)
                for s in range(4):
                    nc.tensor.transpose(bank[:, s * P : (s + 1) * P], words[:, s * P : (s + 1) * P], ident[:])
                banks[i, o] = (b, bank)

        def collect(parts):
            for i, o in parts:
                if i not in turned:
                    turned[i] = stage.tile([P, 2 * K], BF16, name="turned", tag="turned", align_bytes=64)
                b, bank = banks[i, o]
                nc.scalar.copy(
                    out=turned[i][:, o * K : (o + 1) * K].bitcast(F32).rearrange("p (g r u) -> p g r u", g=PASSES, u=2),
                    in_=bank[:].rearrange("p (u g r) -> p g r u", u=2, g=PASSES),
                )
                free_banks.append(b)

        def whole(tiles):
            return [(i, o) for i in tiles for o in BOTH]

        flipped = {}

        def scale_quad(i):
            t = i - TURNED
            dst = stage.tile([P, 2 * K], BF16, name="scaled_quad", tag="scaled_quad", bufs=2, align_bytes=64)
            parts = dst[:].rearrange("p (c u o w e) -> p c o u w e", c=4, u=2, o=2, e=2)
            for c in range(4):
                src = x_quad[c][:, PASSES * P * t : PASSES * P * (t + 1)].rearrange("p (w u e) -> p u w e", u=2, e=2)
                for o in (STYLED, KEPT):
                    col = c * FLIPPED + t
                    nc.scalar.activation(out=parts[:, c, o], in_=src, func=ACT.Copy, scale=share_quad[:, o, col : col + 1])
            scaled[i] = dst

        def flip(i):
            dst = stage.tile([P, K], F32, name="flipped", tag="flipped", bufs=2, align_bytes=64)
            nc.vector.transpose(out=dst[:], in_=scaled[i][:].bitcast(F32))
            flipped[i] = dst

        def regroup(i):
            dst = stage.tile([P, 2 * K], BF16, name="turned", tag="turned", align_bytes=64)
            nc.scalar.copy(
                out=dst[:].bitcast(F32).rearrange("p (v c i u) -> p v c i u", v=4, c=4, u=2),
                in_=flipped[i][:].rearrange("p (c u v i) -> p v c i u", c=4, u=2, v=4),
            )
            turned[i] = dst

        def quantise_x(i, operands=BOTH):
            first, last = operands[0], operands[-1] + 1
            cols = slice(first * PASSES * P, last * PASSES * P)
            nc.vector.quantize_mx(
                out=x_codes[i][:, cols].bitcast(FP8X4), scales=x_scales[i][:, cols], in_=turned[i][:, first * K : last * K]
            )

        def multiply(i, h, o, n0=0, n1=N_HALF):
            if o == STYLED:
                acc_bank[i, h, n0], acc[i, h, n0] = take_bank()
            for g in range(PASSES):
                cols = slice((o * PASSES + g) * P, (o * PASSES + g + 1) * P)
                if o == STYLED:
                    rhs = v_words[h][:, g, 2 * n0 : 2 * n1].bitcast(FP4X4)
                    rhs_scale = v_scales[:, g, h * N_HALF + n0 : h * N_HALF + n1]
                else:
                    rhs = c_codes[g, h][:, n0:n1].bitcast(FP8X4)
                    rhs_scale = c_scales[g, h][:, n0:n1]
                nc.tensor.matmul_mx(
                    out=acc[i, h, n0][:, 0 : n1 - n0],
                    lhsT=x_codes[i][:, cols].bitcast(FP8X4),
                    lhsT_scale=x_scales[i][:, cols],
                    rhs=rhs,
                    rhs_scale=rhs_scale,
                    start=(o == STYLED and g == 0),
                    stop=(o == KEPT and g == PASSES - 1),
                )

        def unit(i, h, n0=0, n1=N_HALF):
            multiply(i, h, STYLED, n0, n1)
            multiply(i, h, KEPT, n0, n1)

        def finish(i, h, n0=0, n1=N_HALF):
            cols = slice(h * N_HALF + n0, h * N_HALF + n1)
            t = stage.tile([P, N_HALF], F32, name="result", tag="result", bufs=16)
            nc.vector.scalar_tensor_tensor(
                out=t[:, 0 : n1 - n0],
                in0=mean_all[:, cols],
                scalar=share[:, STYLED, i : i + 1] if i < TURNED else share_late[:, i - TURNED : i - TURNED + 1],
                in1=acc[i, h, n0][:, 0 : n1 - n0],
                op0=ALU.mult,
                op1=ALU.add,
            )
            free_banks.append(acc_bank[i, h, n0])
            rows = out_turned[:, i, cols] if i < TURNED else out_flipped[:, i - TURNED, cols]
            nc.sync.dma_start(out=rows, in_=t[:, 0 : n1 - n0])

        pieces = [(g, c) for g in range(PASSES) for c in range(0, N_HALF, LATE_PIECE_COLS)]

        def interleave_late(count):
            done = []
            for n in range(min(count, len(pieces))):
                g, c = pieces.pop(0)
                interleave_c(nc.scalar.copy, g, 1, c, c + LATE_PIECE_COLS)
                if c + LATE_PIECE_COLS == N_HALF:
                    done.append(g)
            return done

        S, Kp = (STYLED,), (KEPT,)
        warm_up(WARM_FIRST)
        scale(0, S)
        scale(1, S)
        scale(0, Kp)
        scale(1, Kp)
        turn([(0, STYLED)])
        collect([(0, STYLED)])
        warm_up(WARM_SECOND)
        turn([(1, STYLED), (0, KEPT)])
        collect([(1, STYLED)])
        quantise_x(0, S)
        scale(2)
        quantise_x(1, S)
        collect([(0, KEPT)])
        multiply(0, 0, STYLED)
        interleave_c(nc.vector.tensor_copy, 0, 0, 0, HEAD_VECTOR_COLS)
        interleave_c(nc.scalar.copy, 0, 0, HEAD_VECTOR_COLS, N_HALF)
        turn([(2, STYLED), (1, KEPT), (2, KEPT)])
        spread_mean()
        collect([(2, STYLED)])
        multiply(1, 0, STYLED)
        multiply(0, 1, STYLED)
        multiply(1, 1, STYLED)
        quantise_c(0, 0)
        quantise_x(2, S)
        collect([(1, KEPT)])
        interleave_c(nc.vector.tensor_copy, 1, 0, 0, HEAD_VECTOR_COLS)
        interleave_c(nc.scalar.copy, 1, 0, HEAD_VECTOR_COLS, N_HALF)
        scale(3)
        multiply(2, 0, STYLED)
        multiply(2, 1, STYLED)
        quantise_x(0, Kp)
        quantise_c(1, 0)
        quantise_x(1, Kp)
        collect([(2, KEPT)])
        collect_mean()
        turn(whole([3]))
        collect(whole([3]))
        interleave_late(3)
        quantise_x(2, Kp)
        scale(4)
        multiply(0, 0, KEPT)
        multiply(1, 0, KEPT)
        multiply(2, 0, KEPT)
        finish(0, 0)
        quantise_x(3)
        finish(1, 0)

        first_pair = EARLY + LEAD
        for j in range(EARLY, first_pair):
            turn(whole([j + 1]))
            collect(whole([j + 1]))
            interleave_late(1)
            finish(j - 1, 0)
            unit(j, 0)
            scale(j + 2)
            quantise_x(j + 1)
            if j - EARLY in (1, 4):
                quantise_c((1, 4).index(j - EARLY), 1)
        for i in range(EARLY):
            multiply(i, 1, KEPT)
        finish(first_pair - 1, 0)
        pair = list(range(first_pair + 1, TURNED))
        scale(first_pair + 2)
        finish(0, 1)
        finish(1, 1)
        turn(whole(pair))
        collect(whole(pair))
        make_late_shares()
        scale_quad(TURNED)

        todo = [(first_pair, 0, 0, N_HALF)] + [(i, 1, 0, N_HALF) for i in range(EARLY, first_pair + 1)]
        todo = todo + [(i, h, 0, N_HALF) for i in range(first_pair + 1, TILES) for h in range(HALVES)]
        todo = todo[:-1] + [(TILES - 1, 1, n0, n0 + P) for n0 in range(0, N_HALF, P)]
        last = (EARLY - 1, 1)
        for n, part in enumerate(todo):
            step, phase = divmod(n - FLIP_START, FLIP_PERIOD)
            i = TURNED + step
            if phase == 0 and TURNED <= i < TILES:
                flip(i)
                if i + 1 < TILES:
                    scale_quad(i + 1)
                regroup(i)
            if phase == 0 and TURNED < i <= TILES:
                quantise_x(i - 1)
            unit(*part)
            finish(*last)
            last = part
            if n < len(pair):
                quantise_x(pair[n])
        finish(*last)
